import numpy as np
import ml_dtypes


def mxq(x, axis, fmt="e4m3"):
    dtype, down = {"e4m3": (ml_dtypes.float8_e4m3fn, 7), "e5m2": (ml_dtypes.float8_e5m2, 14)}[fmt]
    v = np.moveaxis(np.asarray(x, np.float32).astype(ml_dtypes.bfloat16).astype(np.float64), axis, -1)
    blocks = v.reshape(v.shape[:-1] + (-1, 32))
    amax = np.abs(blocks).max(-1, keepdims=True)
    byte = np.maximum(np.where(amax > 0, np.frexp(amax)[1] - 1 + 127, 0) - down, 1)
    scale = np.exp2(byte - 127.0)
    codes = (blocks / scale).astype(np.float32).astype(dtype).astype(np.float64)
    return np.moveaxis((codes * scale).reshape(v.shape), -1, axis)


WIDE = False


def mx_kscale(k):
    if not WIDE:
        return np.ones(k)
    levels = np.array([10, -10, 5, -5, 0])
    if k % 512:
        return np.exp2(np.random.permutation(np.resize(levels, k // 32))).repeat(32)
    a = np.empty((k // 512, 16))
    for p in range(k // 512):
        a[p, :8] = np.random.permutation(np.resize(levels, 8))
        for g in range(8):
            far = levels[np.abs(levels - a[p, g]) >= 10]
            a[p, g + 8] = far[np.random.randint(len(far))]
    return np.exp2(a.ravel()).repeat(32)


def f64(x):
    return np.asarray(x).astype(np.float64)


def striped(idx):
    return np.tile(idx.reshape(-1, 16).T, (8, 1)).astype(np.uint16)


def unstriped(offs):
    return offs[:16].T.reshape(-1).astype(np.int64)


E2M1 = np.array([0.0, 0.5, 1.0, 1.5, 2.0, 3.0, 4.0, 6.0, -0.0, -0.5, -1.0, -1.5, -2.0, -3.0, -4.0, -6.0])


def pack_weight(w, fmt):
    k, n = w.shape
    w = f64(np.asarray(w, np.float32).astype(ml_dtypes.bfloat16)).reshape(k // 32, 32, n)
    amax = np.abs(w).max(1)
    if fmt == "e4m3":
        byte = np.frexp(amax)[1] - 1 + 127 - 7
    else:
        mant, ex = np.frexp(amax / 6.0)
        byte = np.where(mant > 0.5, ex, ex - 1) + 127
    byte = np.clip(np.where(amax > 0, byte, 1), 1, 254)
    scaled = (w * np.exp2(127.0 - byte)[:, None, :]).reshape(k, n).astype(np.float32)
    by_word = np.ascontiguousarray(scaled.reshape(k // 512, 128, 4, n).transpose(0, 1, 3, 2))
    if fmt == "e4m3":
        words = by_word.astype(ml_dtypes.float8_e4m3fn).view(np.uint8)
    else:
        c = by_word.astype(ml_dtypes.float4_e2m1fn).view(np.uint8) & 0xF
        words = (c[..., 0::2] | (c[..., 1::2] << 4)).reshape(k // 512, 128, 2 * n)
    return np.ascontiguousarray(words), np.ascontiguousarray(byte.astype(np.uint8).reshape(k // 512, 16, n))


def unpack_weight(words, scales, fmt):
    g, _, n = scales.shape
    words = np.ascontiguousarray(words).reshape(g, 128, n, -1)
    if fmt == "e4m3":
        vals = words.view(ml_dtypes.float8_e4m3fn).astype(np.float64)
    else:
        nib = np.empty((g, 128, n, 4), np.uint8)
        nib[..., 0::2] = words & 0xF
        nib[..., 1::2] = words >> 4
        vals = E2M1[nib]
    vals = vals * np.repeat(np.exp2(scales.astype(np.float64) - 127.0), 8, axis=1)[..., None]
    return vals.transpose(0, 1, 3, 2).reshape(g * 512, n)


def pack_table(v):
    words, scales = pack_weight(v, "e4m3")
    return np.concatenate([words.reshape(words.shape[0], -1), scales.reshape(scales.shape[0], -1)], axis=1)


def unpack_table(tab):
    g, t = tab.shape[0], tab.shape[1] // 528
    return unpack_weight(tab[:, :512 * t].reshape(g, 128, t, 4), tab[:, 512 * t:].reshape(g, 16, t), "e4m3")


def gelu(v):
    return 0.5 * v * (1.0 + np.tanh(np.sqrt(2.0 / np.pi) * (v + 0.044715 * v**3)))


K, M, T, S = 2048, 512, 1024, 512


def setup_inputs():
    n = np.random.standard_normal
    s = mx_kscale(K)[:, None]
    return {
        "tab": pack_table(n((K, T)) * s),
        "w": (n((K, M)) / np.sqrt(K) / s).astype(np.float32),
        "b": (0.3 * n(512)).astype(np.float32),
        "wgo": np.tile(np.random.uniform(0.5, 2.0, S), (128, 1)).astype(np.float32),
        "offs": striped(np.random.permutation(T)[:S]),
        "offs2": striped(np.random.permutation(T)[:S]),
    }


def reference(tab, w, b, wgo, offs, offs2):
    tab_ = unpack_table(tab)[:, unstriped(offs)]
    w_ = mxq(f64(w), 0, "e4m3")
    y = w_.T @ tab_
    out = np.zeros((M, T))
    out[:, unstriped(offs2)] = f64(wgo)[0] * (gelu(y + f64(b)[:, None]))
    return out

@@ -1,0 +1,191 @@
+from contextlib import ExitStack
+
+import concourse.mybir as mybir
+from concourse.masks import make_identity
+
+F32 = mybir.dt.float32
+BF16 = mybir.dt.bfloat16
+I32 = mybir.dt.int32
+U32 = mybir.dt.uint32
+U16 = mybir.dt.uint16
+U8 = mybir.dt.uint8
+FP8X4 = mybir.dt.float8_e4m3fn_x4
+MULT = mybir.AluOpType.mult
+GELU = mybir.ActivationFunctionType.Gelu_apprx_tanh
+
+K, M, T, S = 2048, 512, 1024, 512
+P = 128
+PASSES = K // 512
+FLOPS = 2 * K * M * S
+BYTES = 528 * S * PASSES + 4 * K * M + 4 * M + 4 * S + 4 * P * S // 16 + 4 * M * T
+
+GROUPS = ((0, 128), (128, 256), (256, 512))
+HALF = S // 2
+
+
+def tile_list_tabscat_gelu_kernel(tc, tab, w, b, wgo, offs, offs2, out):
+    nc = tc.nc
+    with ExitStack() as ctx:
+        keep = ctx.enter_context(tc.tile_pool(name="keep", bufs=1))
+        psum = ctx.enter_context(tc.psum_pool(name="psum", bufs=1))
+
+        offs_t = keep.tile([P, S // 16], U16, name="offs_t")
+        offs2_t = keep.tile([P, S // 16], U16, name="offs2_t")
+        tab32 = tab.bitcast(I32)
+
+        planes = keep.tile([P, T], U8, name="planes", align_bytes=64)
+        nc.gpsimd.memset(planes[:].bitcast(I32), 0)
+        wins = []
+        for m in range(4):
+            win = keep.tile([P, T], F32, name=f"win{m}")
+            wins.append(win)
+        nc.vector.memset(wins[0][:], 0.0)
+        nc.vector.memset(wins[1][:], 0.0)
+        nc.gpsimd.memset(wins[2][:], 0.0)
+        nc.gpsimd.memset(wins[3][:], 0.0)
+        warm = keep.tile([P, 1], F32, name="warm")
+        warm2 = keep.tile([P, 1], F32, name="warm2")
+        nc.gpsimd.memset(warm[:], 0.0)
+        nc.scalar.activation(warm2[:], warm[:], GELU)
+
+        words = []
+        raws = {}
+        for a in range(PASSES):
+            tw = keep.tile([P, T], I32, name=f"tab{a}", align_bytes=64)
+            words.append(tw)
+            for g, (c0, c1) in enumerate(GROUPS):
+                rw = keep.tile([P, 4, c1 - c0], F32, name=f"raw{a}_{g}")
+                raws[(a, g)] = rw
+
+        def load_tab(a):
+            nc.sync.dma_start(out=words[a][:], in_=tab32[a, 0 : P * T].rearrange("(p t) -> p t", t=T))
+
+        def load_w(a, g):
+            c0, c1 = GROUPS[g]
+            nc.sync.dma_start(out=raws[(a, g)][:], in_=w[512 * a : 512 * (a + 1), c0:c1].rearrange("(p j) c -> p j c", j=4))
+
+        nc.sync.dma_start(offs_t[:], offs)
+        bias = keep.tile([P, 4], F32, name="bias")
+        brows = keep.tile([P, P], F32, name="brows")
+        ident = keep.tile([P, P], F32, name="ident")
+        nc.gpsimd.memset(brows[:], 0.0)
+        make_identity(nc, ident[:])
+        nc.scalar.dma_start(out=brows[0:4, :], in_=b.rearrange("(m p) -> m p", p=P))
+        bcols = psum.tile([P, P], F32, name="bcols")
+        nc.tensor.transpose(bcols[:], brows[:], ident[:])
+        nc.scalar.copy(out=bias[:], in_=bcols[:, 0:4])
+        wgo_t = keep.tile([P, S], F32, name="wgo_t")
+        load_tab(0)
+        load_w(0, 0)
+        for q in range(4):
+            nc.sync.dma_start(
+                out=planes[32 * q : 32 * q + 16, :].bitcast(I32),
+                in_=tab32[:, P * T + T * q : P * T + T * (q + 1)].rearrange("a (r t) -> a r t", r=4),
+            )
+        load_tab(1)
+        load_w(1, 0)
+        load_tab(2)
+        load_w(2, 0)
+        load_w(3, 0)
+        load_tab(3)
+        nc.sync.dma_start(offs2_t[:], offs2)
+        nc.sync.dma_start(out=wgo_t[:], in_=wgo)
+        for g in range(1, len(GROUPS)):
+            for a in range(PASSES):
+                load_w(a, g)
+
+        gscales = keep.tile([P, S], U8, name="gscales", align_bytes=64)
+        gwords = []
+        for a in range(PASSES):
+            gw = keep.tile([P, S], U32, name=f"gw{a}", align_bytes=64)
+            gwords.append(gw)
+
+        accs = []
+        for m in range(4):
+            row = []
+            for h in range(2 if m == 0 else 1):
+                acc = psum.tile([P, HALF if m == 0 else S], F32, name=f"acc{m}_{h}")
+                row.append(acc)
+            accs.append(row)
+
+        codes = {}
+        scales = {}
+
+        def quantise(a, g):
+            c0, c1 = GROUPS[g]
+            width = c1 - c0
+            grouped = keep.tile([P, width, 4], BF16, name=f"grp{a}_{g}", tag=f"grp{a}_{g}", align_bytes=64)
+            nc.scalar.copy(
+                out=grouped[:].rearrange("p (c i) j -> p c j i", i=4),
+                in_=raws[(a, g)][:].rearrange("p j (c i) -> p c j i", i=4),
+            )
+            cd = keep.tile([P, width], U32, name=f"cd{a}_{g}", align_bytes=64)
+            sc = keep.tile([P, width], U8, name=f"sc{a}_{g}", align_bytes=64)
+            nc.vector.quantize_mx(out=cd[:].bitcast(FP8X4), scales=sc[:], in_=grouped[:].rearrange("p c j -> p (c j)"))
+            codes[(a, g)] = cd
+            scales[(a, g)] = sc
+
+        def gather(a, h0, h1):
+            nc.vector.tensor_copy(gwords[a][:, h0:h1], words[a][:].bitcast(U32).indirect(offs_t[:, h0 // 16 : h1 // 16]))
+
+        def multiply(a, g, h):
+            c0, c1 = GROUPS[g]
+            for m in range(c0 // P, c1 // P):
+                cols = slice(m * P - c0, (m + 1) * P - c0)
+                toks = slice(h * HALF, (h + 1) * HALF) if m == 0 else slice(0, S)
+                nc.tensor.matmul_mx(
+                    out=accs[m][h][:],
+                    lhsT=codes[(a, g)][:, cols].bitcast(FP8X4),
+                    lhsT_scale=scales[(a, g)][:, cols],
+                    rhs=gwords[a][:, toks].bitcast(FP8X4),
+                    rhs_scale=gscales[4 * a : P, toks],
+                    start=(a == 0),
+                    stop=(a == PASSES - 1),
+                )
+
+        acts = {}
+
+        def gelu(m, h):
+            if m < 2:
+                tag = ("grp2_1", "grp2_2")[m] if h else f"act{m}_0"
+                act = keep.tile([P, HALF], F32, name=f"act{m}_{h}", tag=tag, align_bytes=64)
+                acc = accs[0][h][:] if m == 0 else accs[m][0][:, h * HALF : (h + 1) * HALF]
+            else:
+                act = keep.tile([P, S], F32, name=f"act{m}_{h}", align_bytes=64)
+                acc = accs[m][0][:]
+            nc.scalar.activation(act[:], acc, GELU, bias=bias[:, m : m + 1])
+            acts[(m, h)] = act
+
+        def scatter(m, h):
+            cols = slice(h * HALF, (h + 1) * HALF if m < 2 else S)
+            ocols = slice(cols.start // 16, cols.stop // 16)
+            nc.vector.tensor_tensor(wins[m][:].indirect(offs2_t[:, ocols]), acts[(m, h)][:], wgo_t[:, cols], MULT)
+
+        def store(m):
+            nc.sync.dma_start(out=out[m * P : (m + 1) * P, :], in_=wins[m][:])
+
+        for a in range(PASSES):
+            quantise(a, 0)
+            if a < PASSES - 1:
+                gather(a, 0, S)
+                if a == 0:
+                    nc.vector.tensor_copy(gscales[:], planes[:].indirect(offs_t[:]))
+            else:
+                gather(a, 0, HALF)
+                gather(a, HALF, S)
+            multiply(a, 0, 0)
+            multiply(a, 0, 1)
+        gelu(0, 0)
+        for g in range(1, len(GROUPS)):
+            for a in range(PASSES):
+                quantise(a, g)
+                multiply(a, g, 0)
+                if a == 2:
+                    gelu(g - 1, 1)
+            gelu(g, 0)
+        gelu(3, 0)
+        for m in range(4):
+            scatter(m, 0)
+            if m < 2:
+                scatter(m, 1)
+            store(m)

@@ -1,7 +1,6 @@
 from contextlib import ExitStack
 
 import concourse.mybir as mybir
-from concourse.masks import make_identity
 
 F32 = mybir.dt.float32
 BF16 = mybir.dt.bfloat16
@@ -16,10 +15,9 @@ GELU = mybir.ActivationFunctionType.Gelu_apprx_tanh
 K, M, T, S = 2048, 512, 1024, 512
 P = 128
 PASSES = K // 512
+TILES = M // P
 FLOPS = 2 * K * M * S
 BYTES = 528 * S * PASSES + 4 * K * M + 4 * M + 4 * S + 4 * P * S // 16 + 4 * M * T
-
-GROUPS = ((0, 128), (128, 256), (256, 512))
 HALF = S // 2
 
 
@@ -34,65 +32,58 @@ def tile_list_tabscat_gelu_kernel(tc, tab, w, b, wgo, offs, offs2, out):
         tab32 = tab.bitcast(I32)
 
         planes = keep.tile([P, T], U8, name="planes", align_bytes=64)
-        nc.gpsimd.memset(planes[:].bitcast(I32), 0)
-        wins = []
-        for m in range(4):
-            win = keep.tile([P, T], F32, name=f"win{m}")
-            wins.append(win)
-        nc.vector.memset(wins[0][:], 0.0)
-        nc.vector.memset(wins[1][:], 0.0)
-        nc.gpsimd.memset(wins[2][:], 0.0)
-        nc.gpsimd.memset(wins[3][:], 0.0)
+        nc.vector.memset(planes[:].bitcast(I32), 0)
+        brows = keep.tile([P, 32], F32, name="brows", align_bytes=64)
+        bias = keep.tile([P, 32], F32, name="bias", align_bytes=64)
+        nc.vector.memset(brows[:], 0.0)
         warm = keep.tile([P, 1], F32, name="warm")
-        warm2 = keep.tile([P, 1], F32, name="warm2")
-        nc.gpsimd.memset(warm[:], 0.0)
-        nc.scalar.activation(warm2[:], warm[:], GELU)
+        nc.scalar.activation(warm[:], brows[:, 0:1], GELU)
+        wins = []
+        for m in range(3):
+            win = keep.tile([P, T], F32, name=f"win{m}")
+            nc.vector.memset(win[:], 0.0)
+            wins.append(win)
 
         words = []
         raws = {}
         for a in range(PASSES):
             tw = keep.tile([P, T], I32, name=f"tab{a}", align_bytes=64)
             words.append(tw)
-            for g, (c0, c1) in enumerate(GROUPS):
-                rw = keep.tile([P, 4, c1 - c0], F32, name=f"raw{a}_{g}")
-                raws[(a, g)] = rw
+            for m in range(TILES):
+                rw = keep.tile([P, 4, P], F32, name=f"raw{a}_{m}", tag=f"raw{a}_{m}", align_bytes=64)
+                raws[(a, m)] = rw
 
         def load_tab(a):
             nc.sync.dma_start(out=words[a][:], in_=tab32[a, 0 : P * T].rearrange("(p t) -> p t", t=T))
 
-        def load_w(a, g):
-            c0, c1 = GROUPS[g]
-            nc.sync.dma_start(out=raws[(a, g)][:], in_=w[512 * a : 512 * (a + 1), c0:c1].rearrange("(p j) c -> p j c", j=4))
+        def load_w(a, m):
+            nc.sync.dma_start(
+                out=raws[(a, m)][:],
+                in_=w[512 * a : 512 * (a + 1), m * P : (m + 1) * P].rearrange("(p j) c -> p j c", j=4),
+            )
 
-        nc.sync.dma_start(offs_t[:], offs)
-        bias = keep.tile([P, 4], F32, name="bias")
-        brows = keep.tile([P, P], F32, name="brows")
-        ident = keep.tile([P, P], F32, name="ident")
-        nc.gpsimd.memset(brows[:], 0.0)
-        make_identity(nc, ident[:])
-        nc.scalar.dma_start(out=brows[0:4, :], in_=b.rearrange("(m p) -> m p", p=P))
-        bcols = psum.tile([P, P], F32, name="bcols")
-        nc.tensor.transpose(bcols[:], brows[:], ident[:])
-        nc.scalar.copy(out=bias[:], in_=bcols[:, 0:4])
         wgo_t = keep.tile([P, S], F32, name="wgo_t")
+        nc.sync.dma_start(offs_t[:], offs)
         load_tab(0)
-        load_w(0, 0)
         for q in range(4):
             nc.sync.dma_start(
                 out=planes[32 * q : 32 * q + 16, :].bitcast(I32),
                 in_=tab32[:, P * T + T * q : P * T + T * (q + 1)].rearrange("a (r t) -> a r t", r=4),
             )
+        load_w(0, 0)
         load_tab(1)
         load_w(1, 0)
+        nc.sync.dma_start(out=brows[0:P:8, :], in_=b.rearrange("(m q c) -> q m c", q=4, c=32))
         load_tab(2)
         load_w(2, 0)
         load_w(3, 0)
         load_tab(3)
         nc.sync.dma_start(offs2_t[:], offs2)
         nc.sync.dma_start(out=wgo_t[:], in_=wgo)
-        for g in range(1, len(GROUPS)):
+        for m in range(1, TILES):
             for a in range(PASSES):
-                load_w(a, g)
+                load_w(a, m)
+        nc.vector.transpose(bias[:], brows[:])
 
         gscales = keep.tile([P, S], U8, name="gscales", align_bytes=64)
         gwords = []
@@ -100,69 +91,49 @@ def tile_list_tabscat_gelu_kernel(tc, tab, w, b, wgo, offs, offs2, out):
             gw = keep.tile([P, S], U32, name=f"gw{a}", align_bytes=64)
             gwords.append(gw)
 
-        accs = []
-        for m in range(4):
-            row = []
-            for h in range(2 if m == 0 else 1):
-                acc = psum.tile([P, HALF if m == 0 else S], F32, name=f"acc{m}_{h}")
-                row.append(acc)
-            accs.append(row)
-
         codes = {}
         scales = {}
 
-        def quantise(a, g):
-            c0, c1 = GROUPS[g]
-            width = c1 - c0
-            grouped = keep.tile([P, width, 4], BF16, name=f"grp{a}_{g}", tag=f"grp{a}_{g}", align_bytes=64)
+        def quantise(a, m):
+            grouped = keep.tile([P, P, 4], BF16, name=f"grp{a}_{m}", align_bytes=64)
             nc.scalar.copy(
                 out=grouped[:].rearrange("p (c i) j -> p c j i", i=4),
-                in_=raws[(a, g)][:].rearrange("p j (c i) -> p c j i", i=4),
+                in_=raws[(a, m)][:].rearrange("p j (c i) -> p c j i", i=4),
             )
-            cd = keep.tile([P, width], U32, name=f"cd{a}_{g}", align_bytes=64)
-            sc = keep.tile([P, width], U8, name=f"sc{a}_{g}", align_bytes=64)
+            cd = keep.tile([P, P], U32, name=f"cd{a}_{m}", align_bytes=64)
+            sc = keep.tile([P, P], U8, name=f"sc{a}_{m}", align_bytes=64)
             nc.vector.quantize_mx(out=cd[:].bitcast(FP8X4), scales=sc[:], in_=grouped[:].rearrange("p c j -> p (c j)"))
-            codes[(a, g)] = cd
-            scales[(a, g)] = sc
+            codes[(a, m)] = cd
+            scales[(a, m)] = sc
 
         def gather(a, h0, h1):
             nc.vector.tensor_copy(gwords[a][:, h0:h1], words[a][:].bitcast(U32).indirect(offs_t[:, h0 // 16 : h1 // 16]))
 
-        def multiply(a, g, h):
-            c0, c1 = GROUPS[g]
-            for m in range(c0 // P, c1 // P):
-                cols = slice(m * P - c0, (m + 1) * P - c0)
-                toks = slice(h * HALF, (h + 1) * HALF) if m == 0 else slice(0, S)
-                nc.tensor.matmul_mx(
-                    out=accs[m][h][:],
-                    lhsT=codes[(a, g)][:, cols].bitcast(FP8X4),
-                    lhsT_scale=scales[(a, g)][:, cols],
-                    rhs=gwords[a][:, toks].bitcast(FP8X4),
-                    rhs_scale=gscales[4 * a : P, toks],
-                    start=(a == 0),
-                    stop=(a == PASSES - 1),
-                )
+        accs = {}
 
-        acts = {}
+        def multiply(a, m, h):
+            if a == 0:
+                acc = psum.tile([P, HALF], F32, name=f"acc{m}_{h}", tag=(f"first{m}" if h == 0 else "second"))
+                accs[(m, h)] = acc
+            toks = slice(h * HALF, (h + 1) * HALF)
+            nc.tensor.matmul_mx(
+                out=accs[(m, h)][:],
+                lhsT=codes[(a, m)][:].bitcast(FP8X4),
+                lhsT_scale=scales[(a, m)][:],
+                rhs=gwords[a][:, toks].bitcast(FP8X4),
+                rhs_scale=gscales[4 * a : P, toks],
+                start=(a == 0),
+                stop=(a == PASSES - 1),
+            )
 
-        def gelu(m, h):
-            if m < 2:
-                tag = ("grp2_1", "grp2_2")[m] if h else f"act{m}_0"
-                act = keep.tile([P, HALF], F32, name=f"act{m}_{h}", tag=tag, align_bytes=64)
-                acc = accs[0][h][:] if m == 0 else accs[m][0][:, h * HALF : (h + 1) * HALF]
-            else:
-                act = keep.tile([P, S], F32, name=f"act{m}_{h}", align_bytes=64)
-                acc = accs[m][0][:]
-            nc.scalar.activation(act[:], acc, GELU, bias=bias[:, m : m + 1])
-            acts[(m, h)] = act
-
-        def scatter(m, h):
-            cols = slice(h * HALF, (h + 1) * HALF if m < 2 else S)
-            ocols = slice(cols.start // 16, cols.stop // 16)
-            nc.vector.tensor_tensor(wins[m][:].indirect(offs2_t[:, ocols]), acts[(m, h)][:], wgo_t[:, cols], MULT)
-
-        def store(m):
-            nc.sync.dma_start(out=out[m * P : (m + 1) * P, :], in_=wins[m][:])
+        def finish(m, h):
+            tag = f"raw3_{m + 1}" if h == 1 and m + 1 < TILES else f"act{m}_{h}"
+            act = keep.tile([P, HALF], F32, name=f"act{m}_{h}", tag=tag, align_bytes=64)
+            nc.scalar.activation(act[:], accs[(m, h)][:], GELU, bias=bias[:, 8 * m : 8 * m + 1])
+            cols = slice(h * HALF, (h + 1) * HALF)
+            nc.vector.tensor_tensor(wins[m % 3][:].indirect(offs2_t[:, cols.start // 16 : cols.stop // 16]), act[:], wgo_t[:, cols], MULT)
+            if h == 1:
+                nc.sync.dma_start(out=out[m * P : (m + 1) * P, :], in_=wins[m % 3][:])
 
         for a in range(PASSES):
             quantise(a, 0)
@@ -175,17 +146,13 @@ def tile_list_tabscat_gelu_kernel(tc, tab, w, b, wgo, offs, offs2, out):
                 gather(a, HALF, S)
             multiply(a, 0, 0)
             multiply(a, 0, 1)
-        gelu(0, 0)
-        for g in range(1, len(GROUPS)):
+        finish(0, 0)
+        for m in range(1, TILES):
             for a in range(PASSES):
-                quantise(a, g)
-                multiply(a, g, 0)
-                if a == 2:
-                    gelu(g - 1, 1)
-            gelu(g, 0)
-        gelu(3, 0)
-        for m in range(4):
-            scatter(m, 0)
-            if m < 2:
-                scatter(m, 1)
-            store(m)
+                quantise(a, m)
+                multiply(a, m, 0)
+            finish(m - 1, 1)
+            for a in range(PASSES):
+                multiply(a, m, 1)
+            finish(m, 0)
+        finish(TILES - 1, 1)

@@ -1,6 +1,7 @@
 from contextlib import ExitStack
 
 import concourse.mybir as mybir
+from concourse.masks import make_identity
 
 F32 = mybir.dt.float32
 BF16 = mybir.dt.bfloat16
@@ -19,6 +20,7 @@ TILES = M // P
 FLOPS = 2 * K * M * S
 BYTES = 528 * S * PASSES + 4 * K * M + 4 * M + 4 * S + 4 * P * S // 16 + 4 * M * T
 HALF = S // 2
+QUARTER = S // 4
 
 
 def tile_list_tabscat_gelu_kernel(tc, tab, w, b, wgo, offs, offs2, out):
@@ -33,15 +35,12 @@ def tile_list_tabscat_gelu_kernel(tc, tab, w, b, wgo, offs, offs2, out):
 
         planes = keep.tile([P, T], U8, name="planes", align_bytes=64)
         nc.vector.memset(planes[:].bitcast(I32), 0)
-        brows = keep.tile([P, 32], F32, name="brows", align_bytes=64)
-        bias = keep.tile([P, 32], F32, name="bias", align_bytes=64)
-        nc.vector.memset(brows[:], 0.0)
-        warm = keep.tile([P, 1], F32, name="warm")
-        nc.scalar.activation(warm[:], brows[:, 0:1], GELU)
+        brows = keep.tile([P, P], F32, name="brows")
+        nc.gpsimd.memset(brows[:], 0.0)
         wins = []
         for m in range(3):
             win = keep.tile([P, T], F32, name=f"win{m}")
-            nc.vector.memset(win[:], 0.0)
+            (nc.gpsimd if m == 2 else nc.vector).memset(win[:], 0.0)
             wins.append(win)
 
         words = []
@@ -62,28 +61,36 @@ def tile_list_tabscat_gelu_kernel(tc, tab, w, b, wgo, offs, offs2, out):
                 in_=w[512 * a : 512 * (a + 1), m * P : (m + 1) * P].rearrange("(p j) c -> p j c", j=4),
             )
 
-        wgo_t = keep.tile([P, S], F32, name="wgo_t")
+        wcol = keep.tile([P, 4], F32, name="wcol")
+        ident = keep.tile([P, P], F32, name="ident")
+        make_identity(nc, ident[:])
+        warm = keep.tile([P, 1], F32, name="warm")
+        nc.scalar.activation(warm[:], brows[:, 0:1], GELU)
         nc.sync.dma_start(offs_t[:], offs)
         load_tab(0)
+        load_w(0, 0)
         for q in range(4):
             nc.sync.dma_start(
                 out=planes[32 * q : 32 * q + 16, :].bitcast(I32),
                 in_=tab32[:, P * T + T * q : P * T + T * (q + 1)].rearrange("a (r t) -> a r t", r=4),
             )
-        load_w(0, 0)
         load_tab(1)
         load_w(1, 0)
-        nc.sync.dma_start(out=brows[0:P:8, :], in_=b.rearrange("(m q c) -> q m c", q=4, c=32))
+        nc.sync.dma_start(out=brows[0:TILES, :], in_=b.rearrange("(m p) -> m p", p=P))
+        nc.sync.dma_start(out=wcol[:], in_=wgo[0, :].rearrange("(p i) -> p i", i=4))
         load_tab(2)
         load_w(2, 0)
         load_w(3, 0)
         load_tab(3)
         nc.sync.dma_start(offs2_t[:], offs2)
-        nc.sync.dma_start(out=wgo_t[:], in_=wgo)
         for m in range(1, TILES):
             for a in range(PASSES):
                 load_w(a, m)
-        nc.vector.transpose(bias[:], brows[:])
+        bcols = psum.tile([P, P], F32, name="bcols")
+        nc.tensor.transpose(bcols[:], brows[:], ident[:])
+        spread = psum.tile([P, 4, P], F32, name="spread")
+        for i in range(4):
+            nc.tensor.transpose(spread[:, i, :], wcol[:, i : i + 1].to_broadcast([P, P]), ident[:])
 
         gscales = keep.tile([P, S], U8, name="gscales", align_bytes=64)
         gwords = []
@@ -93,50 +100,67 @@ def tile_list_tabscat_gelu_kernel(tc, tab, w, b, wgo, offs, offs2, out):
 
         codes = {}
         scales = {}
+        groups = {}
 
-        def quantise(a, m):
-            grouped = keep.tile([P, P, 4], BF16, name=f"grp{a}_{m}", align_bytes=64)
-            nc.scalar.copy(
-                out=grouped[:].rearrange("p (c i) j -> p c j i", i=4),
+        def interleave(a, n, m):
+            a0 = a - a % n
+            if a == a0:
+                grouped = keep.tile([P, n * P * 4], BF16, name=f"grp{a0}_{m}", align_bytes=64)
+                groups[(a0, m)] = grouped
+            u = a - a0
+            copy = nc.vector.tensor_copy if (a, m) == (0, 1) else nc.scalar.copy
+            copy(
+                out=groups[(a0, m)][:, u * P * 4 : (u + 1) * P * 4].rearrange("p (c i j) -> p c j i", i=4, j=4),
                 in_=raws[(a, m)][:].rearrange("p j (c i) -> p c j i", i=4),
             )
-            cd = keep.tile([P, P], U32, name=f"cd{a}_{m}", align_bytes=64)
-            sc = keep.tile([P, P], U8, name=f"sc{a}_{m}", align_bytes=64)
-            nc.vector.quantize_mx(out=cd[:].bitcast(FP8X4), scales=sc[:], in_=grouped[:].rearrange("p c j -> p (c j)"))
-            codes[(a, m)] = cd
-            scales[(a, m)] = sc
 
-        def gather(a, h0, h1):
-            nc.vector.tensor_copy(gwords[a][:, h0:h1], words[a][:].bitcast(U32).indirect(offs_t[:, h0 // 16 : h1 // 16]))
+        def quantise(a0, n, m):
+            cd = keep.tile([P, n * P], U32, name=f"cd{a0}_{m}", align_bytes=64)
+            sc = keep.tile([P, n * P], U8, name=f"sc{a0}_{m}", align_bytes=64)
+            nc.vector.quantize_mx(out=cd[:].bitcast(FP8X4), scales=sc[:], in_=groups[(a0, m)][:])
+            for u in range(n):
+                codes[(a0 + u, m)] = cd[:, u * P : (u + 1) * P]
+                scales[(a0 + u, m)] = sc[:, u * P : (u + 1) * P]
+
+        def gather(a, j0, j1):
+            nc.vector.tensor_copy(gwords[a][:, j0:j1], words[a][:].bitcast(U32).indirect(offs_t[:, j0 // 16 : j1 // 16]))
 
         accs = {}
 
-        def multiply(a, m, h):
+        def multiply(a, m, j0, j1):
             if a == 0:
-                acc = psum.tile([P, HALF], F32, name=f"acc{m}_{h}", tag=(f"first{m}" if h == 0 else "second"))
-                accs[(m, h)] = acc
-            toks = slice(h * HALF, (h + 1) * HALF)
+                acc = psum.tile([P, j1 - j0], F32, name=f"acc{m}_{j0}", tag=(f"first{m % 2}" if j0 == 0 else f"second{m == 2}"))
+                accs[(m, j0)] = acc
             nc.tensor.matmul_mx(
-                out=accs[(m, h)][:],
-                lhsT=codes[(a, m)][:].bitcast(FP8X4),
-                lhsT_scale=scales[(a, m)][:],
-                rhs=gwords[a][:, toks].bitcast(FP8X4),
-                rhs_scale=gscales[4 * a : P, toks],
+                out=accs[(m, j0)][:],
+                lhsT=codes[(a, m)].bitcast(FP8X4),
+                lhsT_scale=scales[(a, m)],
+                rhs=gwords[a][:, j0:j1].bitcast(FP8X4),
+                rhs_scale=gscales[4 * a : P, j0:j1],
                 start=(a == 0),
                 stop=(a == PASSES - 1),
             )
 
-        def finish(m, h):
-            tag = f"raw3_{m + 1}" if h == 1 and m + 1 < TILES else f"act{m}_{h}"
-            act = keep.tile([P, HALF], F32, name=f"act{m}_{h}", tag=tag, align_bytes=64)
-            nc.scalar.activation(act[:], accs[(m, h)][:], GELU, bias=bias[:, 8 * m : 8 * m + 1])
-            cols = slice(h * HALF, (h + 1) * HALF)
-            nc.vector.tensor_tensor(wins[m % 3][:].indirect(offs2_t[:, cols.start // 16 : cols.stop // 16]), act[:], wgo_t[:, cols], MULT)
-            if h == 1:
+        def gelu(m, act, j0, j1):
+            h = j0 // HALF
+            acc = accs[(m, h * HALF)][:, j0 - h * HALF : j1 - h * HALF]
+            nc.scalar.activation(act, acc, GELU, bias=bias[:, m : m + 1])
+
+        def finish(m, j0, j1, behind):
+            tag = f"act{m}_{j0}" if behind is None else f"raw{behind}_{m + 1}"
+            act = keep.tile([P, j1 - j0], F32, name=f"act{m}_{j0}", tag=tag, align_bytes=64)
+            if j0 < HALF < j1:
+                gelu(m, act[:, 0 : HALF - j0], j0, HALF)
+                gelu(m, act[:, HALF - j0 : j1 - j0], HALF, j1)
+            else:
+                gelu(m, act[:], j0, j1)
+            nc.vector.tensor_tensor(wins[m % 3][:].indirect(offs2_t[:, j0 // 16 : j1 // 16]), act[:], wgo_t[:, j0:j1], MULT)
+            if j1 == S:
                 nc.sync.dma_start(out=out[m * P : (m + 1) * P, :], in_=wins[m % 3][:])
 
         for a in range(PASSES):
-            quantise(a, 0)
+            interleave(a, 1, 0)
+            quantise(a, 1, 0)
             if a < PASSES - 1:
                 gather(a, 0, S)
                 if a == 0:
@@ -144,15 +168,35 @@ def tile_list_tabscat_gelu_kernel(tc, tab, w, b, wgo, offs, offs2, out):
             else:
                 gather(a, 0, HALF)
                 gather(a, HALF, S)
-            multiply(a, 0, 0)
-            multiply(a, 0, 1)
-        finish(0, 0)
-        for m in range(1, TILES):
-            for a in range(PASSES):
-                quantise(a, m)
-                multiply(a, m, 0)
-            finish(m - 1, 1)
-            for a in range(PASSES):
-                multiply(a, m, 1)
-            finish(m, 0)
-        finish(TILES - 1, 1)
+            multiply(a, 0, 0, HALF)
+            multiply(a, 0, HALF, S)
+        bias = keep.tile([P, TILES], F32, name="bias", tag="raw2_0", align_bytes=64)
+        nc.scalar.copy(out=bias[:], in_=bcols[:, 0:TILES])
+        wgo_t = keep.tile([P, S], F32, name="wgo_t", tag="raw3_0", align_bytes=64)
+        nc.scalar.copy(out=wgo_t[:].rearrange("p (c i) -> p c i", i=4), in_=spread[:].rearrange("p i c -> p c i"))
+
+        interleave(0, 2, 1)
+        finish(0, 0, HALF, None)
+        interleave(1, 2, 1)
+        quantise(0, 2, 1)
+        multiply(0, 1, 0, HALF)
+        multiply(1, 1, 0, HALF)
+        for a in (2, 3):
+            interleave(a, 1, 1)
+            quantise(a, 1, 1)
+            multiply(a, 1, 0, HALF)
+        finish(0, HALF, S, 2)
+        for a in range(PASSES):
+            multiply(a, 1, HALF, S)
+
+        for m in range(2, TILES):
+            cut = QUARTER if m == TILES - 1 else HALF
+            for h in range(2):
+                interleave(2 * h, 2, m)
+                interleave(2 * h + 1, 2, m)
+                quantise(2 * h, 2, m)
+                for j0 in (0, HALF):
+                    multiply(2 * h, m, j0, j0 + HALF)
+                    multiply(2 * h + 1, m, j0, j0 + HALF)
+                finish(m - 1, (0, cut)[h], (cut, S)[h], 2 * h)
+        finish(TILES - 1, 0, S, None)

@@ -19,8 +19,10 @@ PASSES = K // 512
 TILES = M // P
 FLOPS = 2 * K * M * S
 BYTES = 528 * S * PASSES + 4 * K * M + 4 * M + 4 * S + 4 * P * S // 16 + 4 * M * T
+
 HALF = S // 2
 QUARTER = S // 4
+WINDOWS = 3
 
 
 def tile_list_tabscat_gelu_kernel(tc, tab, w, b, wgo, offs, offs2, out):
@@ -33,170 +35,184 @@ def tile_list_tabscat_gelu_kernel(tc, tab, w, b, wgo, offs, offs2, out):
         offs2_t = keep.tile([P, S // 16], U16, name="offs2_t")
         tab32 = tab.bitcast(I32)
 
-        planes = keep.tile([P, T], U8, name="planes", align_bytes=64)
-        nc.vector.memset(planes[:].bitcast(I32), 0)
-        brows = keep.tile([P, P], F32, name="brows")
-        nc.gpsimd.memset(brows[:], 0.0)
-        wins = []
-        for m in range(3):
-            win = keep.tile([P, T], F32, name=f"win{m}")
-            (nc.gpsimd if m == 2 else nc.vector).memset(win[:], 0.0)
-            wins.append(win)
+        scale_rows = keep.tile([P, T], U8, name="scale_rows", align_bytes=64)
+        nc.vector.memset(scale_rows[:].bitcast(I32), 0)
+        bias_rows = keep.tile([P, P], F32, name="bias_rows")
+        nc.gpsimd.memset(bias_rows[:], 0.0)
+        windows = []
+        for u in range(WINDOWS):
+            window = keep.tile([P, T], F32, name=f"window{u}")
+            (nc.gpsimd if u == WINDOWS - 1 else nc.vector).memset(window[:], 0.0)
+            windows.append(window)
 
         words = []
         raws = {}
         for a in range(PASSES):
-            tw = keep.tile([P, T], I32, name=f"tab{a}", align_bytes=64)
-            words.append(tw)
+            table_words = keep.tile([P, T], I32, name=f"tab{a}", align_bytes=64)
+            words.append(table_words)
             for m in range(TILES):
-                rw = keep.tile([P, 4, P], F32, name=f"raw{a}_{m}", tag=f"raw{a}_{m}", align_bytes=64)
-                raws[(a, m)] = rw
+                raw = keep.tile([P, 4, P], F32, name=f"raw{a}_{m}", tag=f"raw{a}_{m}", align_bytes=64)
+                raws[(a, m)] = raw
 
-        def load_tab(a):
+        def load_words(a):
             nc.sync.dma_start(out=words[a][:], in_=tab32[a, 0 : P * T].rearrange("(p t) -> p t", t=T))
 
         def load_w(a, m):
             nc.sync.dma_start(
                 out=raws[(a, m)][:],
-                in_=w[512 * a : 512 * (a + 1), m * P : (m + 1) * P].rearrange("(p j) c -> p j c", j=4),
+                in_=w[512 * a : 512 * (a + 1), m * P : (m + 1) * P].rearrange("(p i) c -> p i c", i=4),
             )
 
-        wcol = keep.tile([P, 4], F32, name="wcol")
+        wgo_cols = keep.tile([P, 4], F32, name="wgo_cols")
         ident = keep.tile([P, P], F32, name="ident")
         make_identity(nc, ident[:])
         warm = keep.tile([P, 1], F32, name="warm")
-        nc.scalar.activation(warm[:], brows[:, 0:1], GELU)
+        nc.scalar.activation(warm[:], bias_rows[:, 0:1], GELU)
+
         nc.sync.dma_start(offs_t[:], offs)
-        load_tab(0)
+        load_words(0)
         load_w(0, 0)
-        for q in range(4):
+        for quadrant in range(4):
             nc.sync.dma_start(
-                out=planes[32 * q : 32 * q + 16, :].bitcast(I32),
-                in_=tab32[:, P * T + T * q : P * T + T * (q + 1)].rearrange("a (r t) -> a r t", r=4),
+                out=scale_rows[32 * quadrant : 32 * quadrant + 16, :].bitcast(I32),
+                in_=tab32[:, P * T + T * quadrant : P * T + T * (quadrant + 1)].rearrange("a (r t) -> a r t", r=4),
             )
-        load_tab(1)
+        load_words(1)
         load_w(1, 0)
-        nc.sync.dma_start(out=brows[0:TILES, :], in_=b.rearrange("(m p) -> m p", p=P))
-        nc.sync.dma_start(out=wcol[:], in_=wgo[0, :].rearrange("(p i) -> p i", i=4))
-        load_tab(2)
+        nc.sync.dma_start(out=bias_rows[0:TILES, :], in_=b.rearrange("(m p) -> m p", p=P))
+        nc.sync.dma_start(out=wgo_cols[:], in_=wgo[0, :].rearrange("(p i) -> p i", i=4))
+        load_words(2)
         load_w(2, 0)
         load_w(3, 0)
-        load_tab(3)
+        load_words(3)
+        load_w(0, 1)
+        load_w(1, 1)
         nc.sync.dma_start(offs2_t[:], offs2)
-        for m in range(1, TILES):
+        load_w(2, 1)
+        load_w(3, 1)
+        for m in range(2, TILES):
             for a in range(PASSES):
                 load_w(a, m)
-        bcols = psum.tile([P, P], F32, name="bcols")
-        nc.tensor.transpose(bcols[:], brows[:], ident[:])
+
+        bias_cols = psum.tile([P, P], F32, name="bias_cols")
+        nc.tensor.transpose(bias_cols[:], bias_rows[:], ident[:])
         spread = psum.tile([P, 4, P], F32, name="spread")
         for i in range(4):
-            nc.tensor.transpose(spread[:, i, :], wcol[:, i : i + 1].to_broadcast([P, P]), ident[:])
+            nc.tensor.transpose(spread[:, i, :], wgo_cols[:, i : i + 1].to_broadcast([P, P]), ident[:])
 
-        gscales = keep.tile([P, S], U8, name="gscales", align_bytes=64)
-        gwords = []
+        picked_scales = keep.tile([P, S], U8, name="picked_scales", align_bytes=64)
+        picked_words = []
         for a in range(PASSES):
-            gw = keep.tile([P, S], U32, name=f"gw{a}", align_bytes=64)
-            gwords.append(gw)
+            picked = keep.tile([P, S], U32, name=f"picked{a}", align_bytes=64)
+            picked_words.append(picked)
 
+        rounded = {}
         codes = {}
         scales = {}
-        groups = {}
+        sums = {}
 
-        def interleave(a, n, m):
+        def interleave(a, n, m, copy):
             a0 = a - a % n
             if a == a0:
-                grouped = keep.tile([P, n * P * 4], BF16, name=f"grp{a0}_{m}", align_bytes=64)
-                groups[(a0, m)] = grouped
+                side_by_side = keep.tile([P, n * P * 4], BF16, name=f"rounded{a0}_{m}", align_bytes=64)
+                rounded[(a0, m)] = side_by_side
             u = a - a0
-            copy = nc.vector.tensor_copy if (a, m) == (0, 1) else nc.scalar.copy
             copy(
-                out=groups[(a0, m)][:, u * P * 4 : (u + 1) * P * 4].rearrange("p (c i j) -> p c j i", i=4, j=4),
-                in_=raws[(a, m)][:].rearrange("p j (c i) -> p c j i", i=4),
+                out=rounded[(a0, m)][:, u * P * 4 : (u + 1) * P * 4].rearrange("p (g c i) -> p g i c", c=4, i=4),
+                in_=raws[(a, m)][:].rearrange("p i (g c) -> p g i c", c=4),
             )
 
         def quantise(a0, n, m):
-            cd = keep.tile([P, n * P], U32, name=f"cd{a0}_{m}", align_bytes=64)
-            sc = keep.tile([P, n * P], U8, name=f"sc{a0}_{m}", align_bytes=64)
-            nc.vector.quantize_mx(out=cd[:].bitcast(FP8X4), scales=sc[:], in_=groups[(a0, m)][:])
+            code_tile = keep.tile([P, n * P], U32, name=f"codes{a0}_{m}", align_bytes=64)
+            scale_tile = keep.tile([P, n * P], U8, name=f"scales{a0}_{m}", align_bytes=64)
+            nc.vector.quantize_mx(out=code_tile[:].bitcast(FP8X4), scales=scale_tile[:], in_=rounded[(a0, m)][:])
             for u in range(n):
-                codes[(a0 + u, m)] = cd[:, u * P : (u + 1) * P]
-                scales[(a0 + u, m)] = sc[:, u * P : (u + 1) * P]
+                codes[(a0 + u, m)] = code_tile[:, u * P : (u + 1) * P]
+                scales[(a0 + u, m)] = scale_tile[:, u * P : (u + 1) * P]
 
-        def gather(a, j0, j1):
-            nc.vector.tensor_copy(gwords[a][:, j0:j1], words[a][:].bitcast(U32).indirect(offs_t[:, j0 // 16 : j1 // 16]))
+        def gather_words(a, j0, j1):
+            window = words[a][:].bitcast(U32)
+            nc.vector.tensor_copy(picked_words[a][:, j0:j1], window.indirect(offs_t[:, j0 // 16 : j1 // 16]))
 
-        accs = {}
-
-        def multiply(a, m, j0, j1):
+        def multiply(a, m, h):
             if a == 0:
-                acc = psum.tile([P, j1 - j0], F32, name=f"acc{m}_{j0}", tag=(f"first{m % 2}" if j0 == 0 else f"second{m == 2}"))
-                accs[(m, j0)] = acc
+                bank = f"first{m % 2}" if h == 0 else f"second{m == 2}"
+                half_sums = psum.tile([P, HALF], F32, name=f"sums{m}_{h}", tag=bank)
+                sums[(m, h)] = half_sums
+            entries = slice(h * HALF, (h + 1) * HALF)
             nc.tensor.matmul_mx(
-                out=accs[(m, j0)][:],
+                out=sums[(m, h)][:],
                 lhsT=codes[(a, m)].bitcast(FP8X4),
                 lhsT_scale=scales[(a, m)],
-                rhs=gwords[a][:, j0:j1].bitcast(FP8X4),
-                rhs_scale=gscales[4 * a : P, j0:j1],
+                rhs=picked_words[a][:, entries].bitcast(FP8X4),
+                rhs_scale=picked_scales[4 * a : P, entries],
                 start=(a == 0),
                 stop=(a == PASSES - 1),
             )
 
-        def gelu(m, act, j0, j1):
-            h = j0 // HALF
-            acc = accs[(m, h * HALF)][:, j0 - h * HALF : j1 - h * HALF]
-            nc.scalar.activation(act, acc, GELU, bias=bias[:, m : m + 1])
+        def multiply_pair(a0, m):
+            for h in range(2):
+                multiply(a0, m, h)
+                multiply(a0 + 1, m, h)
 
         def finish(m, j0, j1, behind):
             tag = f"act{m}_{j0}" if behind is None else f"raw{behind}_{m + 1}"
             act = keep.tile([P, j1 - j0], F32, name=f"act{m}_{j0}", tag=tag, align_bytes=64)
-            if j0 < HALF < j1:
-                gelu(m, act[:, 0 : HALF - j0], j0, HALF)
-                gelu(m, act[:, HALF - j0 : j1 - j0], HALF, j1)
-            else:
-                gelu(m, act[:], j0, j1)
-            nc.vector.tensor_tensor(wins[m % 3][:].indirect(offs2_t[:, j0 // 16 : j1 // 16]), act[:], wgo_t[:, j0:j1], MULT)
+            for h in range(j0 // HALF, (j1 - 1) // HALF + 1):
+                lo, hi = max(j0, h * HALF), min(j1, (h + 1) * HALF)
+                nc.scalar.activation(
+                    act[:, lo - j0 : hi - j0],
+                    sums[(m, h)][:, lo - h * HALF : hi - h * HALF],
+                    GELU,
+                    bias=bias[:, m : m + 1],
+                )
+            window = windows[m % WINDOWS]
+            nc.vector.tensor_tensor(window[:].indirect(offs2_t[:, j0 // 16 : j1 // 16]), act[:], wgo_t[:, j0:j1], MULT)
             if j1 == S:
-                nc.sync.dma_start(out=out[m * P : (m + 1) * P, :], in_=wins[m % 3][:])
+                nc.sync.dma_start(out=out[m * P : (m + 1) * P, :], in_=window[:])
 
         for a in range(PASSES):
-            interleave(a, 1, 0)
+            interleave(a, 1, 0, nc.scalar.copy)
             quantise(a, 1, 0)
             if a < PASSES - 1:
-                gather(a, 0, S)
+                gather_words(a, 0, S)
                 if a == 0:
-                    nc.vector.tensor_copy(gscales[:], planes[:].indirect(offs_t[:]))
+                    nc.vector.tensor_copy(picked_scales[:], scale_rows[:].indirect(offs_t[:]))
             else:
-                gather(a, 0, HALF)
-                gather(a, HALF, S)
-            multiply(a, 0, 0, HALF)
-            multiply(a, 0, HALF, S)
+                gather_words(a, 0, HALF)
+                gather_words(a, HALF, S)
+            multiply(a, 0, 0)
+            multiply(a, 0, 1)
         bias = keep.tile([P, TILES], F32, name="bias", tag="raw2_0", align_bytes=64)
-        nc.scalar.copy(out=bias[:], in_=bcols[:, 0:TILES])
+        nc.scalar.copy(out=bias[:], in_=bias_cols[:, 0:TILES])
         wgo_t = keep.tile([P, S], F32, name="wgo_t", tag="raw3_0", align_bytes=64)
         nc.scalar.copy(out=wgo_t[:].rearrange("p (c i) -> p c i", i=4), in_=spread[:].rearrange("p i c -> p c i"))
 
-        interleave(0, 2, 1)
-        finish(0, 0, HALF, None)
-        interleave(1, 2, 1)
-        quantise(0, 2, 1)
-        multiply(0, 1, 0, HALF)
-        multiply(1, 1, 0, HALF)
-        for a in (2, 3):
-            interleave(a, 1, 1)
+        for a in range(PASSES):
+            interleave(a, 1, 1, nc.vector.tensor_copy if a == 0 else nc.scalar.copy)
             quantise(a, 1, 1)
-            multiply(a, 1, 0, HALF)
+            if a == 0:
+                finish(0, 0, HALF, None)
+            multiply(a, 1, 0)
         finish(0, HALF, S, 2)
         for a in range(PASSES):
-            multiply(a, 1, HALF, S)
+            multiply(a, 1, 1)
 
-        for m in range(2, TILES):
-            cut = QUARTER if m == TILES - 1 else HALF
-            for h in range(2):
-                interleave(2 * h, 2, m)
-                interleave(2 * h + 1, 2, m)
-                quantise(2 * h, 2, m)
-                for j0 in (0, HALF):
-                    multiply(2 * h, m, j0, j0 + HALF)
-                    multiply(2 * h + 1, m, j0, j0 + HALF)
-                finish(m - 1, (0, cut)[h], (cut, S)[h], 2 * h)
-        finish(TILES - 1, 0, S, None)
+        for h in range(2):
+            interleave(2 * h, 2, 2, nc.scalar.copy)
+            interleave(2 * h + 1, 2, 2, nc.scalar.copy)
+            quantise(2 * h, 2, 2)
+            multiply_pair(2 * h, 2)
+            finish(1, h * HALF, (h + 1) * HALF, 2 * h)
+
+        interleave(0, 2, 3, nc.scalar.copy)
+        interleave(1, 2, 3, nc.scalar.copy)
+        quantise(0, 2, 3)
+        multiply_pair(0, 3)
+        interleave(2, 2, 3, nc.scalar.copy)
+        finish(2, 0, QUARTER, 1)
+        interleave(3, 2, 3, nc.scalar.copy)
+        quantise(2, 2, 3)
+        multiply_pair(2, 3)
+        finish(2, QUARTER, S, 2)
+        finish(3, 0, S, None)

@@ -42,7 +42,7 @@ def tile_list_tabscat_gelu_kernel(tc, tab, w, b, wgo, offs, offs2, out):
         windows = []
         for u in range(WINDOWS):
             window = keep.tile([P, T], F32, name=f"window{u}")
-            (nc.gpsimd if u == WINDOWS - 1 else nc.vector).memset(window[:], 0.0)
+            (nc.vector if u == 0 else nc.gpsimd).memset(window[:], 0.0)
             windows.append(window)
 
         words = []
@@ -189,9 +189,9 @@ def tile_list_tabscat_gelu_kernel(tc, tab, w, b, wgo, offs, offs2, out):
         nc.scalar.copy(out=wgo_t[:].rearrange("p (c i) -> p c i", i=4), in_=spread[:].rearrange("p i c -> p c i"))
 
         for a in range(PASSES):
-            interleave(a, 1, 1, nc.vector.tensor_copy if a == 0 else nc.scalar.copy)
+            interleave(a, 1, 1, nc.vector.tensor_copy if a == 1 else nc.scalar.copy)
             quantise(a, 1, 1)
-            if a == 0:
+            if a == 1:
                 finish(0, 0, HALF, None)
             multiply(a, 1, 0)
         finish(0, HALF, S, 2)

@@ -42,7 +42,7 @@ def tile_list_tabscat_gelu_kernel(tc, tab, w, b, wgo, offs, offs2, out):
         windows = []
         for u in range(WINDOWS):
             window = keep.tile([P, T], F32, name=f"window{u}")
-            (nc.vector if u == 0 else nc.gpsimd).memset(window[:], 0.0)
+            (nc.gpsimd if u == WINDOWS - 1 else nc.vector).memset(window[:], 0.0)
             windows.append(window)
 
         words = []
@@ -210,9 +210,8 @@ def tile_list_tabscat_gelu_kernel(tc, tab, w, b, wgo, offs, offs2, out):
         quantise(0, 2, 3)
         multiply_pair(0, 3)
         interleave(2, 2, 3, nc.scalar.copy)
-        finish(2, 0, QUARTER, 1)
         interleave(3, 2, 3, nc.scalar.copy)
         quantise(2, 2, 3)
         multiply_pair(2, 3)
-        finish(2, QUARTER, S, 2)
+        finish(2, 0, S, 2)
         finish(3, 0, S, None)

@@ -21,7 +21,6 @@ FLOPS = 2 * K * M * S
 BYTES = 528 * S * PASSES + 4 * K * M + 4 * M + 4 * S + 4 * P * S // 16 + 4 * M * T
 
 HALF = S // 2
-QUARTER = S // 4
 WINDOWS = 3
 
 
@@ -69,8 +68,8 @@ def tile_list_tabscat_gelu_kernel(tc, tab, w, b, wgo, offs, offs2, out):
         warm = keep.tile([P, 1], F32, name="warm")
         nc.scalar.activation(warm[:], bias_rows[:, 0:1], GELU)
 
-        nc.sync.dma_start(offs_t[:], offs)
         load_words(0)
+        nc.sync.dma_start(offs_t[:], offs)
         load_w(0, 0)
         for quadrant in range(4):
             nc.sync.dma_start(
@@ -131,8 +130,8 @@ def tile_list_tabscat_gelu_kernel(tc, tab, w, b, wgo, offs, offs2, out):
                 scales[(a0 + u, m)] = scale_tile[:, u * P : (u + 1) * P]
 
         def gather_words(a, j0, j1):
-            window = words[a][:].bitcast(U32)
-            nc.vector.tensor_copy(picked_words[a][:, j0:j1], window.indirect(offs_t[:, j0 // 16 : j1 // 16]))
+            table = words[a][:].bitcast(U32)
+            nc.vector.tensor_copy(picked_words[a][:, j0:j1], table.indirect(offs_t[:, j0 // 16 : j1 // 16]))
 
         def multiply(a, m, h):
             if a == 0:
@@ -171,21 +170,26 @@ def tile_list_tabscat_gelu_kernel(tc, tab, w, b, wgo, offs, offs2, out):
             if j1 == S:
                 nc.sync.dma_start(out=out[m * P : (m + 1) * P, :], in_=window[:])
 
-        for a in range(PASSES):
+        interleave(0, 2, 0, nc.scalar.copy)
+        gather_words(0, 0, S)
+        nc.vector.tensor_copy(picked_scales[:], scale_rows[:].indirect(offs_t[:]))
+        interleave(1, 2, 0, nc.scalar.copy)
+        quantise(0, 2, 0)
+        gather_words(1, 0, S)
+        multiply_pair(0, 0)
+        for a in range(2, PASSES):
             interleave(a, 1, 0, nc.scalar.copy)
             quantise(a, 1, 0)
             if a < PASSES - 1:
                 gather_words(a, 0, S)
-                if a == 0:
-                    nc.vector.tensor_copy(picked_scales[:], scale_rows[:].indirect(offs_t[:]))
             else:
                 gather_words(a, 0, HALF)
                 gather_words(a, HALF, S)
             multiply(a, 0, 0)
             multiply(a, 0, 1)
-        bias = keep.tile([P, TILES], F32, name="bias", tag="raw2_0", align_bytes=64)
+        bias = keep.tile([P, TILES], F32, name="bias", tag="raw0_0", align_bytes=64)
         nc.scalar.copy(out=bias[:], in_=bias_cols[:, 0:TILES])
-        wgo_t = keep.tile([P, S], F32, name="wgo_t", tag="raw3_0", align_bytes=64)
+        wgo_t = keep.tile([P, S], F32, name="wgo_t", tag="raw1_0", align_bytes=64)
         nc.scalar.copy(out=wgo_t[:].rearrange("p (c i) -> p c i", i=4), in_=spread[:].rearrange("p i c -> p c i"))
 
         for a in range(PASSES):

@@ -63,6 +63,7 @@ def tile_list_tabscat_gelu_kernel(tc, tab, w, b, wgo, offs, offs2, out):
             )
 
         wgo_cols = keep.tile([P, 4], F32, name="wgo_cols")
+        nc.scalar.dma_start(out=wgo_cols[:], in_=wgo[0, :].rearrange("(p i) -> p i", i=4))
         ident = keep.tile([P, P], F32, name="ident")
         make_identity(nc, ident[:])
         warm = keep.tile([P, 1], F32, name="warm")
@@ -70,16 +71,15 @@ def tile_list_tabscat_gelu_kernel(tc, tab, w, b, wgo, offs, offs2, out):
 
         load_words(0)
         nc.sync.dma_start(offs_t[:], offs)
+        load_words(1)
         load_w(0, 0)
         for quadrant in range(4):
             nc.sync.dma_start(
                 out=scale_rows[32 * quadrant : 32 * quadrant + 16, :].bitcast(I32),
                 in_=tab32[:, P * T + T * quadrant : P * T + T * (quadrant + 1)].rearrange("a (r t) -> a r t", r=4),
             )
-        load_words(1)
         load_w(1, 0)
         nc.sync.dma_start(out=bias_rows[0:TILES, :], in_=b.rearrange("(m p) -> m p", p=P))
-        nc.sync.dma_start(out=wgo_cols[:], in_=wgo[0, :].rearrange("(p i) -> p i", i=4))
         load_words(2)
         load_w(2, 0)
         load_w(3, 0)

@@ -34,7 +34,7 @@ def tile_list_tabscat_gelu_kernel(tc, tab, w, b, wgo, offs, offs2, out):
         offs2_t = keep.tile([P, S // 16], U16, name="offs2_t")
         tab32 = tab.bitcast(I32)
 
-        scale_rows = keep.tile([P, T], U8, name="scale_rows", align_bytes=64)
+        scale_rows = keep.tile([P, 2 * T], U8, name="scale_rows", align_bytes=64)
         nc.vector.memset(scale_rows[:].bitcast(I32), 0)
         bias_rows = keep.tile([P, P], F32, name="bias_rows")
         nc.gpsimd.memset(bias_rows[:], 0.0)
@@ -74,8 +74,10 @@ def tile_list_tabscat_gelu_kernel(tc, tab, w, b, wgo, offs, offs2, out):
         load_words(1)
         load_w(0, 0)
         for quadrant in range(4):
+            first = 32 * (quadrant % 2)
+            column = T * (quadrant // 2)
             nc.sync.dma_start(
-                out=scale_rows[32 * quadrant : 32 * quadrant + 16, :].bitcast(I32),
+                out=scale_rows[first : first + 16, column : column + T].bitcast(I32),
                 in_=tab32[:, P * T + T * quadrant : P * T + T * (quadrant + 1)].rearrange("a (r t) -> a r t", r=4),
             )
         load_w(1, 0)
@@ -172,7 +174,8 @@ def tile_list_tabscat_gelu_kernel(tc, tab, w, b, wgo, offs, offs2, out):
 
         interleave(0, 2, 0, nc.scalar.copy)
         gather_words(0, 0, S)
-        nc.vector.tensor_copy(picked_scales[:], scale_rows[:].indirect(offs_t[:]))
+        nc.vector.tensor_copy(scale_rows[64:P, 0:T].bitcast(I32), scale_rows[0:64, T : 2 * T].bitcast(I32))
+        nc.vector.tensor_copy(picked_scales[:], scale_rows[:, 0:T].indirect(offs_t[:]))
         interleave(1, 2, 0, nc.scalar.copy)
         quantise(0, 2, 0)
         gather_words(1, 0, S)

@@ -34,23 +34,23 @@ def tile_list_tabscat_gelu_kernel(tc, tab, w, b, wgo, offs, offs2, out):
         offs2_t = keep.tile([P, S // 16], U16, name="offs2_t")
         tab32 = tab.bitcast(I32)
 
-        scale_rows = keep.tile([P, 2 * T], U8, name="scale_rows", align_bytes=64)
+        scale_rows = keep.tile([P, 2 * T], U8, name="scale_rows", align_bytes=256)
         nc.vector.memset(scale_rows[:].bitcast(I32), 0)
-        bias_rows = keep.tile([P, P], F32, name="bias_rows")
+        bias_rows = keep.tile([P, P], F32, name="bias_rows", align_bytes=256)
         nc.gpsimd.memset(bias_rows[:], 0.0)
         windows = []
         for u in range(WINDOWS):
-            window = keep.tile([P, T], F32, name=f"window{u}")
+            window = keep.tile([P, T], F32, name=f"window{u}", align_bytes=256)
             (nc.gpsimd if u == WINDOWS - 1 else nc.vector).memset(window[:], 0.0)
             windows.append(window)
 
         words = []
         raws = {}
         for a in range(PASSES):
-            table_words = keep.tile([P, T], I32, name=f"tab{a}", align_bytes=64)
+            table_words = keep.tile([P, T], I32, name=f"tab{a}", align_bytes=256)
             words.append(table_words)
             for m in range(TILES):
-                raw = keep.tile([P, 4, P], F32, name=f"raw{a}_{m}", tag=f"raw{a}_{m}", align_bytes=64)
+                raw = keep.tile([P, 4, P], F32, name=f"raw{a}_{m}", tag=f"raw{a}_{m}", align_bytes=256)
                 raws[(a, m)] = raw
 
         def load_words(a):
@@ -101,10 +101,10 @@ def tile_list_tabscat_gelu_kernel(tc, tab, w, b, wgo, offs, offs2, out):
         for i in range(4):
             nc.tensor.transpose(spread[:, i, :], wgo_cols[:, i : i + 1].to_broadcast([P, P]), ident[:])
 
-        picked_scales = keep.tile([P, S], U8, name="picked_scales", align_bytes=64)
+        picked_scales = keep.tile([P, S], U8, name="picked_scales", align_bytes=256)
         picked_words = []
         for a in range(PASSES):
-            picked = keep.tile([P, S], U32, name=f"picked{a}", align_bytes=64)
+            picked = keep.tile([P, S], U32, name=f"picked{a}", align_bytes=256)
             picked_words.append(picked)
 
         rounded = {}
@@ -115,7 +115,7 @@ def tile_list_tabscat_gelu_kernel(tc, tab, w, b, wgo, offs, offs2, out):
         def interleave(a, n, m, copy):
             a0 = a - a % n
             if a == a0:
-                side_by_side = keep.tile([P, n * P * 4], BF16, name=f"rounded{a0}_{m}", align_bytes=64)
+                side_by_side = keep.tile([P, n * P * 4], BF16, name=f"rounded{a0}_{m}", align_bytes=256)
                 rounded[(a0, m)] = side_by_side
             u = a - a0
             copy(
@@ -124,8 +124,8 @@ def tile_list_tabscat_gelu_kernel(tc, tab, w, b, wgo, offs, offs2, out):
             )
 
         def quantise(a0, n, m):
-            code_tile = keep.tile([P, n * P], U32, name=f"codes{a0}_{m}", align_bytes=64)
-            scale_tile = keep.tile([P, n * P], U8, name=f"scales{a0}_{m}", align_bytes=64)
+            code_tile = keep.tile([P, n * P], U32, name=f"codes{a0}_{m}", align_bytes=256)
+            scale_tile = keep.tile([P, n * P], U8, name=f"scales{a0}_{m}", align_bytes=256)
             nc.vector.quantize_mx(out=code_tile[:].bitcast(FP8X4), scales=scale_tile[:], in_=rounded[(a0, m)][:])
             for u in range(n):
                 codes[(a0 + u, m)] = code_tile[:, u * P : (u + 1) * P]
@@ -158,7 +158,7 @@ def tile_list_tabscat_gelu_kernel(tc, tab, w, b, wgo, offs, offs2, out):
 
         def finish(m, j0, j1, behind):
             tag = f"act{m}_{j0}" if behind is None else f"raw{behind}_{m + 1}"
-            act = keep.tile([P, j1 - j0], F32, name=f"act{m}_{j0}", tag=tag, align_bytes=64)
+            act = keep.tile([P, j1 - j0], F32, name=f"act{m}_{j0}", tag=tag, align_bytes=256)
             for h in range(j0 // HALF, (j1 - 1) // HALF + 1):
                 lo, hi = max(j0, h * HALF), min(j1, (h + 1) * HALF)
                 nc.scalar.activation(
@@ -190,9 +190,9 @@ def tile_list_tabscat_gelu_kernel(tc, tab, w, b, wgo, offs, offs2, out):
                 gather_words(a, HALF, S)
             multiply(a, 0, 0)
             multiply(a, 0, 1)
-        bias = keep.tile([P, TILES], F32, name="bias", tag="raw0_0", align_bytes=64)
+        bias = keep.tile([P, TILES], F32, name="bias", tag="raw0_0", align_bytes=256)
         nc.scalar.copy(out=bias[:], in_=bias_cols[:, 0:TILES])
-        wgo_t = keep.tile([P, S], F32, name="wgo_t", tag="raw1_0", align_bytes=64)
+        wgo_t = keep.tile([P, S], F32, name="wgo_t", tag="raw1_0", align_bytes=256)
         nc.scalar.copy(out=wgo_t[:].rearrange("p (c i) -> p c i", i=4), in_=spread[:].rearrange("p i c -> p c i"))
 
         for a in range(PASSES):

from contextlib import ExitStack

import concourse.mybir as mybir
from concourse.masks import make_identity

F32 = mybir.dt.float32
BF16 = mybir.dt.bfloat16
I32 = mybir.dt.int32
U32 = mybir.dt.uint32
U16 = mybir.dt.uint16
U8 = mybir.dt.uint8
FP8X4 = mybir.dt.float8_e4m3fn_x4
MULT = mybir.AluOpType.mult
GELU = mybir.ActivationFunctionType.Gelu_apprx_tanh

K, M, T, S = 2048, 512, 1024, 512
P = 128
PASSES = K // 512
TILES = M // P
FLOPS = 2 * K * M * S
BYTES = 528 * S * PASSES + 4 * K * M + 4 * M + 4 * S + 4 * P * S // 16 + 4 * M * T

HALF = S // 2
WINDOWS = 3


def tile_list_tabscat_gelu_kernel(tc, tab, w, b, wgo, offs, offs2, out):
    nc = tc.nc
    with ExitStack() as ctx:
        keep = ctx.enter_context(tc.tile_pool(name="keep", bufs=1))
        psum = ctx.enter_context(tc.psum_pool(name="psum", bufs=1))

        offs_t = keep.tile([P, S // 16], U16, name="offs_t")
        offs2_t = keep.tile([P, S // 16], U16, name="offs2_t")
        tab32 = tab.bitcast(I32)

        scale_rows = keep.tile([P, 2 * T], U8, name="scale_rows", align_bytes=256)
        nc.vector.memset(scale_rows[:].bitcast(I32), 0)
        bias_rows = keep.tile([P, P], F32, name="bias_rows", align_bytes=256)
        nc.gpsimd.memset(bias_rows[:], 0.0)
        windows = []
        for u in range(WINDOWS):
            window = keep.tile([P, T], F32, name=f"window{u}", align_bytes=256)
            (nc.gpsimd if u == WINDOWS - 1 else nc.vector).memset(window[:], 0.0)
            windows.append(window)

        words = []
        raws = {}
        for a in range(PASSES):
            table_words = keep.tile([P, T], I32, name=f"tab{a}", align_bytes=256)
            words.append(table_words)
            for m in range(TILES):
                raw = keep.tile([P, 4, P], F32, name=f"raw{a}_{m}", tag=f"raw{a}_{m}", align_bytes=256)
                raws[(a, m)] = raw

        def load_words(a):
            nc.sync.dma_start(out=words[a][:], in_=tab32[a, 0 : P * T].rearrange("(p t) -> p t", t=T))

        def load_w(a, m):
            nc.sync.dma_start(
                out=raws[(a, m)][:],
                in_=w[512 * a : 512 * (a + 1), m * P : (m + 1) * P].rearrange("(p i) c -> p i c", i=4),
            )

        wgo_cols = keep.tile([P, 4], F32, name="wgo_cols")
        nc.scalar.dma_start(out=wgo_cols[:], in_=wgo[0, :].rearrange("(p i) -> p i", i=4))
        ident = keep.tile([P, P], F32, name="ident")
        make_identity(nc, ident[:])
        warm = keep.tile([P, 1], F32, name="warm")
        nc.scalar.activation(warm[:], bias_rows[:, 0:1], GELU)

        load_words(0)
        nc.sync.dma_start(offs_t[:], offs)
        load_words(1)
        load_w(0, 0)
        for quadrant in range(4):
            first = 32 * (quadrant % 2)
            column = T * (quadrant // 2)
            nc.sync.dma_start(
                out=scale_rows[first : first + 16, column : column + T].bitcast(I32),
                in_=tab32[:, P * T + T * quadrant : P * T + T * (quadrant + 1)].rearrange("a (r t) -> a r t", r=4),
            )
        load_w(1, 0)
        nc.sync.dma_start(out=bias_rows[0:TILES, :], in_=b.rearrange("(m p) -> m p", p=P))
        load_words(2)
        load_w(2, 0)
        load_w(3, 0)
        load_words(3)
        load_w(0, 1)
        load_w(1, 1)
        nc.sync.dma_start(offs2_t[:], offs2)
        load_w(2, 1)
        load_w(3, 1)
        for m in range(2, TILES):
            for a in range(PASSES):
                load_w(a, m)

        bias_cols = psum.tile([P, P], F32, name="bias_cols")
        nc.tensor.transpose(bias_cols[:], bias_rows[:], ident[:])
        spread = psum.tile([P, 4, P], F32, name="spread")
        for i in range(4):
            nc.tensor.transpose(spread[:, i, :], wgo_cols[:, i : i + 1].to_broadcast([P, P]), ident[:])

        picked_scales = keep.tile([P, S], U8, name="picked_scales", align_bytes=256)
        picked_words = []
        for a in range(PASSES):
            picked = keep.tile([P, S], U32, name=f"picked{a}", align_bytes=256)
            picked_words.append(picked)

        rounded = {}
        codes = {}
        scales = {}
        sums = {}

        def interleave(a, n, m, copy):
            a0 = a - a % n
            if a == a0:
                side_by_side = keep.tile([P, n * P * 4], BF16, name=f"rounded{a0}_{m}", align_bytes=256)
                rounded[(a0, m)] = side_by_side
            u = a - a0
            copy(
                out=rounded[(a0, m)][:, u * P * 4 : (u + 1) * P * 4].rearrange("p (g c i) -> p g i c", c=4, i=4),
                in_=raws[(a, m)][:].rearrange("p i (g c) -> p g i c", c=4),
            )

        def quantise(a0, n, m):
            code_tile = keep.tile([P, n * P], U32, name=f"codes{a0}_{m}", align_bytes=256)
            scale_tile = keep.tile([P, n * P], U8, name=f"scales{a0}_{m}", align_bytes=256)
            nc.vector.quantize_mx(out=code_tile[:].bitcast(FP8X4), scales=scale_tile[:], in_=rounded[(a0, m)][:])
            for u in range(n):
                codes[(a0 + u, m)] = code_tile[:, u * P : (u + 1) * P]
                scales[(a0 + u, m)] = scale_tile[:, u * P : (u + 1) * P]

        def gather_words(a, j0, j1):
            table = words[a][:].bitcast(U32)
            nc.vector.tensor_copy(picked_words[a][:, j0:j1], table.indirect(offs_t[:, j0 // 16 : j1 // 16]))

        def multiply(a, m, h):
            if a == 0:
                bank = f"first{m % 2}" if h == 0 else f"second{m == 2}"
                half_sums = psum.tile([P, HALF], F32, name=f"sums{m}_{h}", tag=bank)
                sums[(m, h)] = half_sums
            entries = slice(h * HALF, (h + 1) * HALF)
            nc.tensor.matmul_mx(
                out=sums[(m, h)][:],
                lhsT=codes[(a, m)].bitcast(FP8X4),
                lhsT_scale=scales[(a, m)],
                rhs=picked_words[a][:, entries].bitcast(FP8X4),
                rhs_scale=picked_scales[4 * a : P, entries],
                start=(a == 0),
                stop=(a == PASSES - 1),
            )

        def multiply_pair(a0, m):
            for h in range(2):
                multiply(a0, m, h)
                multiply(a0 + 1, m, h)

        def finish(m, j0, j1, behind):
            tag = f"act{m}_{j0}" if behind is None else f"raw{behind}_{m + 1}"
            act = keep.tile([P, j1 - j0], F32, name=f"act{m}_{j0}", tag=tag, align_bytes=256)
            for h in range(j0 // HALF, (j1 - 1) // HALF + 1):
                lo, hi = max(j0, h * HALF), min(j1, (h + 1) * HALF)
                nc.scalar.activation(
                    act[:, lo - j0 : hi - j0],
                    sums[(m, h)][:, lo - h * HALF : hi - h * HALF],
                    GELU,
                    bias=bias[:, m : m + 1],
                )
            window = windows[m % WINDOWS]
            nc.vector.tensor_tensor(window[:].indirect(offs2_t[:, j0 // 16 : j1 // 16]), act[:], wgo_t[:, j0:j1], MULT)
            if j1 == S:
                nc.sync.dma_start(out=out[m * P : (m + 1) * P, :], in_=window[:])

        interleave(0, 2, 0, nc.scalar.copy)
        gather_words(0, 0, S)
        nc.vector.tensor_copy(scale_rows[64:P, 0:T].bitcast(I32), scale_rows[0:64, T : 2 * T].bitcast(I32))
        nc.vector.tensor_copy(picked_scales[:], scale_rows[:, 0:T].indirect(offs_t[:]))
        interleave(1, 2, 0, nc.scalar.copy)
        quantise(0, 2, 0)
        gather_words(1, 0, S)
        multiply_pair(0, 0)
        for a in range(2, PASSES):
            interleave(a, 1, 0, nc.scalar.copy)
            quantise(a, 1, 0)
            if a < PASSES - 1:
                gather_words(a, 0, S)
            else:
                gather_words(a, 0, HALF)
                gather_words(a, HALF, S)
            multiply(a, 0, 0)
            multiply(a, 0, 1)
        bias = keep.tile([P, TILES], F32, name="bias", tag="raw0_0", align_bytes=256)
        nc.scalar.copy(out=bias[:], in_=bias_cols[:, 0:TILES])
        wgo_t = keep.tile([P, S], F32, name="wgo_t", tag="raw1_0", align_bytes=256)
        nc.scalar.copy(out=wgo_t[:].rearrange("p (c i) -> p c i", i=4), in_=spread[:].rearrange("p i c -> p c i"))

        for a in range(PASSES):
            interleave(a, 1, 1, nc.vector.tensor_copy if a == 1 else nc.scalar.copy)
            quantise(a, 1, 1)
            if a == 1:
                finish(0, 0, HALF, None)
            multiply(a, 1, 0)
        finish(0, HALF, S, 2)
        for a in range(PASSES):
            multiply(a, 1, 1)

        for h in range(2):
            interleave(2 * h, 2, 2, nc.scalar.copy)
            interleave(2 * h + 1, 2, 2, nc.scalar.copy)
            quantise(2 * h, 2, 2)
            multiply_pair(2 * h, 2)
            finish(1, h * HALF, (h + 1) * HALF, 2 * h)

        interleave(0, 2, 3, nc.scalar.copy)
        interleave(1, 2, 3, nc.scalar.copy)
        quantise(0, 2, 3)
        multiply_pair(0, 3)
        interleave(2, 2, 3, nc.scalar.copy)
        interleave(3, 2, 3, nc.scalar.copy)
        quantise(2, 2, 3)
        multiply_pair(2, 3)
        finish(2, 0, S, 2)
        finish(3, 0, S, None)
